import numpy as np
import ml_dtypes


def mxq(x, axis, fmt="e4m3"):
    dtype, down = {"e4m3": (ml_dtypes.float8_e4m3fn, 7), "e5m2": (ml_dtypes.float8_e5m2, 14)}[fmt]
    v = np.moveaxis(np.asarray(x, np.float32).astype(ml_dtypes.bfloat16).astype(np.float64), axis, -1)
    blocks = v.reshape(v.shape[:-1] + (-1, 32))
    amax = np.abs(blocks).max(-1, keepdims=True)
    byte = np.maximum(np.where(amax > 0, np.frexp(amax)[1] - 1 + 127, 0) - down, 1)
    scale = np.exp2(byte - 127.0)
    codes = (blocks / scale).astype(np.float32).astype(dtype).astype(np.float64)
    return np.moveaxis((codes * scale).reshape(v.shape), -1, axis)


WIDE = False


def mx_kscale(k):
    if not WIDE:
        return np.ones(k)
    levels = np.array([30, -30])
    if k % 512:
        return np.exp2(np.random.permutation(np.resize(levels, k // 32))).repeat(32)
    a = np.empty((k // 512, 16))
    for p in range(k // 512):
        a[p, :8] = np.random.permutation(np.resize(levels, 8))
        for g in range(8):
            far = levels[np.abs(levels - a[p, g]) >= 10]
            a[p, g + 8] = far[np.random.randint(len(far))]
    return np.exp2(a.ravel()).repeat(32)


def f64(x):
    return np.asarray(x).astype(np.float64)


def striped(idx):
    return np.tile(np.asarray(idx).reshape(-1, 16).T, (8, 1)).astype(np.uint16)


def unstriped(offs):
    return offs[:16].T.reshape(-1).astype(np.int64)


E2M1 = np.array([0.0, 0.5, 1.0, 1.5, 2.0, 3.0, 4.0, 6.0, -0.0, -0.5, -1.0, -1.5, -2.0, -3.0, -4.0, -6.0])


def pack_weight(w, fmt):
    k, n = w.shape
    w = f64(np.asarray(w, np.float32).astype(ml_dtypes.bfloat16)).reshape(k // 32, 32, n)
    amax = np.abs(w).max(1)
    if fmt in ("e4m3", "e5m2"):
        byte = np.frexp(amax)[1] - 1 + 127 - (7 if fmt == "e4m3" else 14)
    else:
        mant, ex = np.frexp(amax / 6.0)
        byte = np.where(mant > 0.5, ex, ex - 1) + 127
    byte = np.clip(np.where(amax > 0, byte, 1), 1, 254)
    scaled = (w * np.exp2(127.0 - byte)[:, None, :]).reshape(k, n).astype(np.float32)
    by_word = np.ascontiguousarray(scaled.reshape(k // 512, 128, 4, n).transpose(0, 1, 3, 2))
    if fmt in ("e4m3", "e5m2"):
        words = by_word.astype(ml_dtypes.float8_e4m3fn if fmt == "e4m3" else ml_dtypes.float8_e5m2).view(np.uint8)
    else:
        c = by_word.astype(ml_dtypes.float4_e2m1fn).view(np.uint8) & 0xF
        words = (c[..., 0::2] | (c[..., 1::2] << 4)).reshape(k // 512, 128, 2 * n)
    return np.ascontiguousarray(words), np.ascontiguousarray(byte.astype(np.uint8).reshape(k // 512, 16, n))


def unpack_weight(words, scales, fmt):
    g, _, n = scales.shape
    words = np.ascontiguousarray(words).reshape(g, 128, n, -1)
    if fmt in ("e4m3", "e5m2"):
        vals = words.view(ml_dtypes.float8_e4m3fn if fmt == "e4m3" else ml_dtypes.float8_e5m2).astype(np.float64)
    else:
        nib = np.empty((g, 128, n, 4), np.uint8)
        nib[..., 0::2] = words & 0xF
        nib[..., 1::2] = words >> 4
        vals = E2M1[nib]
    vals = vals * np.repeat(np.exp2(scales.astype(np.float64) - 127.0), 8, axis=1)[..., None]
    return vals.transpose(0, 1, 3, 2).reshape(g * 512, n)


K, F, T, Z, J, R, C, N, E = 512, 512, 1024, 1024, 256, 512, 512, 256, 1024


def setup_inputs():
    n = np.random.standard_normal
    idx = np.random.permutation(T)[:J]
    idx2 = np.random.permutation(Z)[:J]
    idx3 = np.random.permutation(C)[:J]
    idx4 = np.random.permutation(C)[:J]
    idx5 = np.random.permutation(T)[:J]
    idx6 = np.random.permutation(E)[:J]
    fk = mx_kscale(K)
    fr = mx_kscale(R)
    ff = mx_kscale(F)
    xtp = pack_weight(n((K, T)) / fk[:, None], "e4m3")
    wp = pack_weight(n((K, R)) * 1 / np.sqrt(K) * fk[:, None] * fr, "e2m1")
    xop = pack_weight(n((F, Z)) / ff[:, None], "e2m1")
    w0p = pack_weight(n((F, R)) * 1 / np.sqrt(F) * ff[:, None] * fr, "e5m2")
    wbp = pack_weight(n((R, N)) * 1 / np.sqrt(R) / fr[:, None], "e5m2")
    wsp = pack_weight(n((K, N)) * 1 / np.sqrt(K) * fk[:, None], "e5m2")
    return {
        "xt_words": xtp[0],
        "xt_scales": xtp[1],
        "w_words": wp[0],
        "w_scales": wp[1],
        "xo_words": xop[0],
        "xo_scales": xop[1],
        "w0_words": w0p[0],
        "w0_scales": w0p[1],
        "wb_words": wbp[0],
        "wb_scales": wbp[1],
        "ws_words": wsp[0],
        "ws_scales": wsp[1],
        "tz": (n((N, E))).astype(np.float32),
        "offs": striped(idx),
        "offs2": striped(idx2),
        "offs3": striped(idx3),
        "offs4": striped(idx4),
        "offs5": striped(idx5),
        "offs6": striped(idx6),
    }


def reference(xt_words, xt_scales, w_words, w_scales, xo_words, xo_scales, w0_words, w0_scales, wb_words, wb_scales, ws_words, ws_scales, tz, offs, offs2, offs3, offs4, offs5, offs6):
    idx = unstriped(offs)
    idx2 = unstriped(offs2)
    idx3 = unstriped(offs3)
    idx4 = unstriped(offs4)
    idx5 = unstriped(offs5)
    idx6 = unstriped(offs6)
    xtu = unpack_weight(xt_words, xt_scales, "e4m3")
    wu = unpack_weight(w_words, w_scales, "e2m1")
    xou = unpack_weight(xo_words, xo_scales, "e2m1")
    w0u = unpack_weight(w0_words, w0_scales, "e5m2")
    wbu = unpack_weight(wb_words, wb_scales, "e5m2")
    wsu = unpack_weight(ws_words, ws_scales, "e5m2")
    xtidxg = xtu[:, idx]
    xoidx2g = xou[:, idx2]
    a = wu.T @ xtidxg + w0u.T @ xoidx2g
    pw = np.zeros((R, C))
    pw[:, idx3] = a
    hid = np.abs(pw[:, idx4] - a)
    hidq = mxq(hid, 0, "e4m3")
    xtidx5g = xtu[:, idx5]
    p = wbu.T @ hidq + wsu.T @ xtidx5g
    y = p + f64(tz)[:, idx6]
    return y

@@ -1,0 +1,209 @@
+from contextlib import ExitStack
+
+import concourse.mybir as mybir
+
+K, F, T, Z, J, R, C, N, E = 512, 512, 1024, 1024, 256, 512, 512, 256, 1024
+FLOPS = 2 * J * (K * R + F * R + R * N + K * N)
+
+F32 = mybir.dt.float32
+BF16 = mybir.dt.bfloat16
+I32 = mybir.dt.int32
+U32 = mybir.dt.uint32
+U16 = mybir.dt.uint16
+U8 = mybir.dt.uint8
+E4M3 = mybir.dt.float8_e4m3fn_x4
+E5M2 = mybir.dt.float8_e5m2_x4
+E2M1 = mybir.dt.float4_e2m1fn_x4
+ACT = mybir.ActivationFunctionType
+ALU = mybir.AluOpType
+
+P = 128
+PACK = 4
+ROWS = 16
+TOP = 96
+HALF = J // 2
+
+
+def tile_list_ownboard_bank_further_tabled_kernel(
+    tc, xt_words, xt_scales, w_words, w_scales, xo_words, xo_scales, w0_words, w0_scales,
+    wb_words, wb_scales, ws_words, ws_scales, tz, offs, offs2, offs3, offs4, offs5, offs6, out,
+):
+    nc = tc.nc
+
+    def words32(ap):
+        return ap[0].rearrange("p n t -> p (n t)").bitcast(I32)
+
+    def twice(ap):
+        rows = ap[0].bitcast(I32)
+        return rows.unsqueeze(1).to_broadcast([ROWS, 2, rows.shape[1]])
+
+    with ExitStack() as ctx:
+        lists = ctx.enter_context(tc.tile_pool(name="lists", bufs=1))
+        sb = ctx.enter_context(tc.tile_pool(name="sb", bufs=1))
+        psum = ctx.enter_context(tc.psum_pool(name="psum", bufs=1))
+
+        def new(name, shape, dtype, tag=None):
+            return sb.tile(shape, dtype, name=name, tag=tag or name, align_bytes=64)
+
+        def load_list(name, ap):
+            tile = lists.tile([P, J // 16], U16, name=name)
+            nc.sync.dma_start(tile[:], ap)
+            return tile
+
+        xt_s = new("xt_s", [P, T], U8)
+        xo_s = new("xo_s", [P, Z], U8)
+        w_raw = new("w_raw", [P, 2, R], U8)
+        xt_w = new("xt_w", [P, T], U32)
+        xo_w = new("xo_w", [P, Z], U16)
+        w_w = new("w_w", [P, R], U16)
+        w0_w = new("w0_w", [P, R], U32)
+        wb_w = new("wb_w", [P, N], U32)
+        ws_w = new("ws_w", [P, N], U32)
+        tz_t = [new("tz%d" % c, [P, E], F32) for c in range(2)]
+        stage1 = new("stage1", [P, 2 * J + 2 * R], U8)
+        plane1 = new("plane1", [P, 2 * J + 2 * R], U8)
+        stage2 = new("stage2", [P, J + 2 * N], U8)
+        plane2 = new("plane2", [P, J + 2 * N], U8)
+        board = [new("board%d" % t, [P, C], F32) for t in range(2)]
+
+        l1 = load_list("l1", offs)
+        nc.sync.dma_start(xt_s[TOP:P, :].bitcast(I32), twice(xt_scales))
+        l2 = load_list("l2", offs2)
+        nc.sync.dma_start(xo_s[TOP:P, :].bitcast(I32), twice(xo_scales))
+        nc.sync.dma_start(w_raw[TOP:P, 0, :].bitcast(I32), twice(w_scales))
+        nc.sync.dma_start(w_raw[TOP:P, 1, :].bitcast(I32), twice(w0_scales))
+        nc.scalar.dma_start(xt_w[:].bitcast(I32), words32(xt_words))
+        nc.scalar.dma_start(w0_w[:].bitcast(I32), words32(w0_words))
+        l5 = load_list("l5", offs5)
+        l3 = load_list("l3", offs3)
+        nc.sync.dma_start(w_w[:].bitcast(I32), w_words[0].bitcast(I32))
+        nc.sync.dma_start(xo_w[:].bitcast(I32), xo_words[0].bitcast(I32))
+        l6 = load_list("l6", offs6)
+        l4 = load_list("l4", offs4)
+        nc.gpsimd.dma_start(stage2[TOP:P:2, J : J + N].bitcast(I32), wb_scales[0].bitcast(I32))
+        nc.gpsimd.dma_start(stage2[TOP:P:2, J + N :].bitcast(I32), ws_scales[0].bitcast(I32))
+        for c in range(2):
+            nc.gpsimd.dma_start(tz_t[c][:], tz[c * P : (c + 1) * P, :])
+        nc.gpsimd.dma_start(ws_w[:].bitcast(I32), words32(ws_words))
+        nc.gpsimd.dma_start(wb_w[:].bitcast(I32), words32(wb_words))
+
+        nc.vector.memset(xt_s[0:TOP, :].bitcast(I32), 0)
+        nc.vector.memset(xo_s[0:TOP, :].bitcast(I32), 0)
+        nc.vector.memset(w_raw[0:TOP].rearrange("p w r -> p (w r)").bitcast(I32), 0)
+        nc.vector.memset(plane1[:].bitcast(I32), 0)
+        for t in range(2):
+            nc.vector.memset(board[t][:], 0.0)
+        nc.vector.memset(plane2[:].bitcast(I32), 0)
+
+        def gather(name, window, offsets, dtype):
+            tile = new(name, [P, J], dtype)
+            nc.vector.tensor_copy(tile[:], window[:].indirect(offsets[:]))
+            return tile
+
+        def deal(plane, stage):
+            for q in range(4):
+                nc.sync.dma_start(
+                    plane[32 * q : 32 * q + 4, :].bitcast(I32),
+                    stage[TOP + 8 * q : TOP + 8 * q + 8 : 2, :].bitcast(I32),
+                )
+
+        g_xt_s = gather("g_xt_s", xt_s, l1, U8)
+        g_xo_s = gather("g_xo_s", xo_s, l2, U8)
+        nc.vector.tensor_copy(stage1[TOP:P, 0:J].bitcast(I32), g_xt_s[TOP:P, :].bitcast(I32))
+        nc.vector.tensor_copy(
+            stage1[:, 2 * J :].rearrange("p (w t m) -> p w t m", w=2, t=PACK),
+            w_raw[:].rearrange("p w (m t) -> p w t m", t=PACK),
+        )
+        nc.vector.tensor_copy(stage1[TOP:P, J : 2 * J].bitcast(I32), g_xo_s[TOP:P, :].bitcast(I32))
+        deal(plane1, stage1)
+
+        g_xt_w = gather("g_xt_w", xt_w, l1, U32)
+        g_xo_w = gather("g_xo_w", xo_w, l2, U16)
+
+        w0_p = new("w0_p", [P, R], U32)
+        w_p = new("w_p", [P, R], U16)
+        nc.scalar.copy(w0_p[:].rearrange("p (t m) -> p m t", t=PACK), w0_w[:].rearrange("p (m t) -> p m t", t=PACK))
+        nc.scalar.copy(w_p[:].rearrange("p (t m) -> p m t", t=PACK), w_w[:].rearrange("p (m t) -> p m t", t=PACK))
+
+        a_ps = []
+        for t in range(PACK):
+            acc = psum.tile([P, J], F32, name="a_ps%d" % t)
+            cols = slice(t * P, (t + 1) * P)
+            nc.tensor.matmul_mx(
+                acc[:], lhsT=w_p[:, cols].bitcast(E2M1), lhsT_scale=plane1[:, 2 * J + t * P : 2 * J + (t + 1) * P],
+                rhs=g_xt_w[:].bitcast(E4M3), rhs_scale=plane1[:, 0:J], start=True, stop=False,
+            )
+            nc.tensor.matmul_mx(
+                acc[:], lhsT=w0_p[:, cols].bitcast(E5M2),
+                lhsT_scale=plane1[:, 2 * J + R + t * P : 2 * J + R + (t + 1) * P],
+                rhs=g_xo_w[:].bitcast(E2M1), rhs_scale=plane1[:, J : 2 * J], start=False, stop=True,
+            )
+            a_ps.append(acc)
+
+        g5_s = gather("g5_s", xt_s, l5, U8)
+        g5_w = gather("g5_w", xt_w, l5, U32)
+        nc.vector.tensor_copy(stage2[TOP:P, 0:J].bitcast(I32), g5_s[TOP:P, :].bitcast(I32))
+        deal(plane2, stage2)
+
+        board.append(new("board2", [P, C], F32, tag="w_raw"))
+        board.append(new("board3", [P, C], F32, tag="stage1"))
+        for t in range(2, PACK):
+            nc.vector.memset(board[t][:], 0.0)
+
+        tz_g = new("tz_g", [P, 2, J], F32)
+        nc.vector.tensor_copy(tz_g[:, 0, :], tz_t[0][:].indirect(l6[:]))
+        nc.vector.tensor_copy(tz_g[:, 1, :], tz_t[1][:].indirect(l6[:]))
+
+        p_ps = [psum.tile([P, 2, HALF], F32, name="p_ps%d" % h) for h in range(2)]
+        for h in range(2):
+            js = slice(h * HALF, (h + 1) * HALF)
+            for c in range(2):
+                nc.tensor.matmul_mx(
+                    p_ps[h][:, c, :], lhsT=ws_w[:, c * P : (c + 1) * P].bitcast(E5M2),
+                    lhsT_scale=plane2[:, J + N + c * P : J + N + (c + 1) * P],
+                    rhs=g5_w[:, js].bitcast(E4M3), rhs_scale=plane2[:, js], start=(c == 0), stop=False,
+                )
+
+        a_sb = [new("a_sb%d" % t, [P, J], F32) for t in range(PACK)]
+        diff = new("diff", [P, PACK, J], F32)
+
+        def put_scalar(t):
+            nc.scalar.activation(board[t][:].indirect(l3[:]), a_sb[t][:], ACT.Copy)
+
+        def look(t):
+            nc.vector.tensor_tensor(diff[:, t, :], board[t][:].indirect(l4[:]), a_sb[t][:], ALU.subtract)
+
+        nc.scalar.copy(a_sb[0][:], a_ps[0][:])
+        put_scalar(0)
+        nc.vector.tensor_copy(a_sb[1][:], a_ps[1][:])
+        nc.vector.tensor_copy(a_sb[2][:], a_ps[2][:])
+        nc.vector.tensor_copy(board[1][:].indirect(l3[:]), a_sb[1][:])
+        nc.scalar.copy(a_sb[3][:], a_ps[3][:])
+        put_scalar(2)
+        put_scalar(3)
+        for t in range(PACK - 1):
+            look(t)
+
+        out_v = out.rearrange("(c p) j -> p c j", p=P)
+        for h in range(2):
+            js = slice(h * HALF, (h + 1) * HALF)
+            nc.vector.tensor_tensor(
+                diff[:, PACK - 1, js], board[PACK - 1][:].indirect(l4[:, h * 8 : (h + 1) * 8]),
+                a_sb[PACK - 1][:, js], ALU.subtract,
+            )
+        for h in range(2):
+            js = slice(h * HALF, (h + 1) * HALF)
+            hid = new("hid%d" % h, [P, HALF, PACK], BF16)
+            nc.scalar.activation(hid[:], diff[:, :, js].rearrange("p t j -> p j t"), ACT.Abs)
+            hq = new("hq%d" % h, [P, HALF], U32)
+            hs = new("hs%d" % h, [P, HALF], U8)
+            nc.vector.quantize_mx(hq[:].bitcast(E4M3), hs[:], hid[:].rearrange("p j t -> p (j t)"))
+            for c in range(2):
+                nc.tensor.matmul_mx(
+                    p_ps[h][:, c, :], lhsT=wb_w[:, c * P : (c + 1) * P].bitcast(E5M2),
+                    lhsT_scale=plane2[:, J + c * P : J + (c + 1) * P],
+                    rhs=hq[:].bitcast(E4M3), rhs_scale=hs[:], start=False, stop=(c == 1),
+                )
+            res = new("res%d" % h, [P, 2, HALF], F32)
+            nc.vector.tensor_tensor(res[:], p_ps[h][:], tz_g[:, :, js], ALU.add)
+            nc.sync.dma_start(out_v[:, :, js], res[:])

@@ -59,100 +59,100 @@ def tile_list_ownboard_bank_further_tabled_kernel(
         w0_w = new("w0_w", [P, R], U32)
         wb_w = new("wb_w", [P, N], U32)
         ws_w = new("ws_w", [P, N], U32)
-        tz_t = [new("tz%d" % c, [P, E], F32) for c in range(2)]
-        stage1 = new("stage1", [P, 2 * J + 2 * R], U8)
-        plane1 = new("plane1", [P, 2 * J + 2 * R], U8)
+        stage1 = new("stage1", [P, 2 * J + R], U8)
+        plane1 = new("plane1", [P, 2 * J + R], U8)
+        plane1b = new("plane1b", [P, R], U8)
         stage2 = new("stage2", [P, J + 2 * N], U8)
         plane2 = new("plane2", [P, J + 2 * N], U8)
-        board = [new("board%d" % t, [P, C], F32) for t in range(2)]
+        board = [new("board%d" % t, [P, C], F32) for t in range(PACK)]
 
-        l1 = load_list("l1", offs)
-        nc.sync.dma_start(xt_s[TOP:P, :].bitcast(I32), twice(xt_scales))
-        l2 = load_list("l2", offs2)
-        nc.sync.dma_start(xo_s[TOP:P, :].bitcast(I32), twice(xo_scales))
-        nc.sync.dma_start(w_raw[TOP:P, 0, :].bitcast(I32), twice(w_scales))
-        nc.sync.dma_start(w_raw[TOP:P, 1, :].bitcast(I32), twice(w0_scales))
-        nc.scalar.dma_start(xt_w[:].bitcast(I32), words32(xt_words))
-        nc.scalar.dma_start(w0_w[:].bitcast(I32), words32(w0_words))
-        l5 = load_list("l5", offs5)
-        l3 = load_list("l3", offs3)
-        nc.sync.dma_start(w_w[:].bitcast(I32), w_words[0].bitcast(I32))
-        nc.sync.dma_start(xo_w[:].bitcast(I32), xo_words[0].bitcast(I32))
-        l6 = load_list("l6", offs6)
-        l4 = load_list("l4", offs4)
-        nc.gpsimd.dma_start(stage2[TOP:P:2, J : J + N].bitcast(I32), wb_scales[0].bitcast(I32))
-        nc.gpsimd.dma_start(stage2[TOP:P:2, J + N :].bitcast(I32), ws_scales[0].bitcast(I32))
-        for c in range(2):
-            nc.gpsimd.dma_start(tz_t[c][:], tz[c * P : (c + 1) * P, :])
-        nc.gpsimd.dma_start(ws_w[:].bitcast(I32), words32(ws_words))
-        nc.gpsimd.dma_start(wb_w[:].bitcast(I32), words32(wb_words))
-
-        nc.vector.memset(xt_s[0:TOP, :].bitcast(I32), 0)
-        nc.vector.memset(xo_s[0:TOP, :].bitcast(I32), 0)
-        nc.vector.memset(w_raw[0:TOP].rearrange("p w r -> p (w r)").bitcast(I32), 0)
+        nc.gpsimd.memset(xt_s[0:TOP, :].bitcast(I32), 0)
+        nc.gpsimd.memset(xo_s[0:TOP, :].bitcast(I32), 0)
+        nc.gpsimd.memset(w_raw[0:TOP].rearrange("p w r -> p (w r)").bitcast(I32), 0)
         nc.vector.memset(plane1[:].bitcast(I32), 0)
+        nc.vector.memset(plane1b[:].bitcast(I32), 0)
         for t in range(2):
             nc.vector.memset(board[t][:], 0.0)
-        nc.vector.memset(plane2[:].bitcast(I32), 0)
+
+        l1 = load_list("l1", offs)
+        nc.scalar.dma_start(xt_s[TOP:P, :].bitcast(I32), twice(xt_scales))
+        nc.sync.dma_start(w_raw[TOP:P, 0, :].bitcast(I32), twice(w_scales))
+        nc.scalar.dma_start(xo_s[TOP:P, :].bitcast(I32), twice(xo_scales))
+        l2 = load_list("l2", offs2)
+        nc.scalar.dma_start(w_raw[TOP:P, 1, :].bitcast(I32), twice(w0_scales))
+        nc.sync.dma_start(xt_w[:].bitcast(I32), words32(xt_words))
+        nc.scalar.dma_start(w_w[:].bitcast(I32), w_words[0].bitcast(I32))
+        nc.sync.dma_start(w0_w[:].bitcast(I32), words32(w0_words))
+        nc.sync.dma_start(xo_w[:].bitcast(I32), xo_words[0].bitcast(I32))
+        l5 = load_list("l5", offs5)
+        l3 = load_list("l3", offs3)
+        nc.gpsimd.dma_start(stage2[TOP:P:2, J : J + N].bitcast(I32), wb_scales[0].bitcast(I32))
+        nc.gpsimd.dma_start(stage2[TOP:P:2, J + N :].bitcast(I32), ws_scales[0].bitcast(I32))
+        for t in range(2, PACK):
+            nc.gpsimd.memset(board[t][:], 0.0)
+        nc.gpsimd.dma_start(ws_w[:].bitcast(I32), words32(ws_words))
+        nc.gpsimd.dma_start(wb_w[:].bitcast(I32), words32(wb_words))
+        nc.gpsimd.memset(plane2[:].bitcast(I32), 0)
 
         def gather(name, window, offsets, dtype):
             tile = new(name, [P, J], dtype)
             nc.vector.tensor_copy(tile[:], window[:].indirect(offsets[:]))
             return tile
 
-        def deal(plane, stage):
+        def deal(plane, stage, queues):
             for q in range(4):
-                nc.sync.dma_start(
+                queues[q % len(queues)].dma_start(
                     plane[32 * q : 32 * q + 4, :].bitcast(I32),
                     stage[TOP + 8 * q : TOP + 8 * q + 8 : 2, :].bitcast(I32),
                 )
 
-        g_xt_s = gather("g_xt_s", xt_s, l1, U8)
-        g_xo_s = gather("g_xo_s", xo_s, l2, U8)
-        nc.vector.tensor_copy(stage1[TOP:P, 0:J].bitcast(I32), g_xt_s[TOP:P, :].bitcast(I32))
-        nc.vector.tensor_copy(
-            stage1[:, 2 * J :].rearrange("p (w t m) -> p w t m", w=2, t=PACK),
-            w_raw[:].rearrange("p w (m t) -> p w t m", t=PACK),
-        )
-        nc.vector.tensor_copy(stage1[TOP:P, J : 2 * J].bitcast(I32), g_xo_s[TOP:P, :].bitcast(I32))
-        deal(plane1, stage1)
+        w_p = new("w_p", [P, R], U16)
+        nc.scalar.copy(w_p[:].rearrange("p (t m) -> p m t", t=PACK), w_w[:].rearrange("p (m t) -> p m t", t=PACK))
+        by_t = w_raw[:].rearrange("p w (m t) -> p w t m", t=PACK)
+        g_s = new("g_s", [P, 2 * J], U8)
+        nc.vector.tensor_copy(g_s[:, 0:J], xt_s[:].indirect(l1[:]))
+        nc.vector.tensor_copy(g_s[:, J:], xo_s[:].indirect(l2[:]))
+        nc.vector.tensor_copy(stage1[:, 2 * J :].rearrange("p (w t m) -> p w t m", w=2, t=2), by_t[:, :, 0:2, :])
+        nc.vector.tensor_copy(stage1[:, 0 : 2 * J].bitcast(I32), g_s[:].bitcast(I32))
+        deal(plane1, stage1, (nc.scalar, nc.sync))
+        stage1b = new("stage1b", [P, R], U8, tag="g_s")
+        nc.vector.tensor_copy(stage1b[:].rearrange("p (w t m) -> p w t m", w=2, t=2), by_t[:, :, 2:4, :])
+        deal(plane1b, stage1b, (nc.sync,))
+        tz_t = new("tz_t", [P, 2, E], F32)
+        nc.sync.dma_start(tz_t[:, 1, :], tz[P : 2 * P, :])
+        l6 = load_list("l6", offs6)
+        l4 = load_list("l4", offs4)
+        nc.sync.dma_start(tz_t[:, 0, :], tz[0:P, :])
 
         g_xt_w = gather("g_xt_w", xt_w, l1, U32)
         g_xo_w = gather("g_xo_w", xo_w, l2, U16)
 
         w0_p = new("w0_p", [P, R], U32)
-        w_p = new("w_p", [P, R], U16)
         nc.scalar.copy(w0_p[:].rearrange("p (t m) -> p m t", t=PACK), w0_w[:].rearrange("p (m t) -> p m t", t=PACK))
-        nc.scalar.copy(w_p[:].rearrange("p (t m) -> p m t", t=PACK), w_w[:].rearrange("p (m t) -> p m t", t=PACK))
+
+        def w_plane(which, t):
+            at = which * 2 * P + (t % 2) * P
+            return plane1[:, 2 * J + at : 2 * J + at + P] if t < 2 else plane1b[:, at : at + P]
 
         a_ps = []
         for t in range(PACK):
             acc = psum.tile([P, J], F32, name="a_ps%d" % t)
             cols = slice(t * P, (t + 1) * P)
             nc.tensor.matmul_mx(
-                acc[:], lhsT=w_p[:, cols].bitcast(E2M1), lhsT_scale=plane1[:, 2 * J + t * P : 2 * J + (t + 1) * P],
+                acc[:], lhsT=w_p[:, cols].bitcast(E2M1), lhsT_scale=w_plane(0, t),
                 rhs=g_xt_w[:].bitcast(E4M3), rhs_scale=plane1[:, 0:J], start=True, stop=False,
             )
             nc.tensor.matmul_mx(
                 acc[:], lhsT=w0_p[:, cols].bitcast(E5M2),
-                lhsT_scale=plane1[:, 2 * J + R + t * P : 2 * J + R + (t + 1) * P],
+                lhsT_scale=w_plane(1, t),
                 rhs=g_xo_w[:].bitcast(E2M1), rhs_scale=plane1[:, J : 2 * J], start=False, stop=True,
             )
             a_ps.append(acc)
 
         g5_s = gather("g5_s", xt_s, l5, U8)
         g5_w = gather("g5_w", xt_w, l5, U32)
-        nc.vector.tensor_copy(stage2[TOP:P, 0:J].bitcast(I32), g5_s[TOP:P, :].bitcast(I32))
-        deal(plane2, stage2)
-
-        board.append(new("board2", [P, C], F32, tag="w_raw"))
-        board.append(new("board3", [P, C], F32, tag="stage1"))
-        for t in range(2, PACK):
-            nc.vector.memset(board[t][:], 0.0)
-
-        tz_g = new("tz_g", [P, 2, J], F32)
-        nc.vector.tensor_copy(tz_g[:, 0, :], tz_t[0][:].indirect(l6[:]))
-        nc.vector.tensor_copy(tz_g[:, 1, :], tz_t[1][:].indirect(l6[:]))
+        nc.vector.tensor_copy(stage2[:, 0:J].bitcast(I32), g5_s[:].bitcast(I32))
+        deal(plane2, stage2, (nc.sync,))
 
         p_ps = [psum.tile([P, 2, HALF], F32, name="p_ps%d" % h) for h in range(2)]
         for h in range(2):
@@ -176,14 +176,16 @@ def tile_list_ownboard_bank_further_tabled_kernel(
         nc.scalar.copy(a_sb[0][:], a_ps[0][:])
         put_scalar(0)
         nc.vector.tensor_copy(a_sb[1][:], a_ps[1][:])
-        nc.vector.tensor_copy(a_sb[2][:], a_ps[2][:])
         nc.vector.tensor_copy(board[1][:].indirect(l3[:]), a_sb[1][:])
-        nc.scalar.copy(a_sb[3][:], a_ps[3][:])
+        nc.scalar.copy(a_sb[2][:], a_ps[2][:])
         put_scalar(2)
+        nc.vector.tensor_copy(a_sb[3][:], a_ps[3][:])
         put_scalar(3)
         for t in range(PACK - 1):
             look(t)
 
+        tz_g = new("tz_g", [P, 2, J], F32, tag="board2")
+        nc.scalar.activation(tz_g[:, 1, :], tz_t[:, 1, :].indirect(l6[:]), ACT.Copy)
         out_v = out.rearrange("(c p) j -> p c j", p=P)
         for h in range(2):
             js = slice(h * HALF, (h + 1) * HALF)
@@ -191,10 +193,14 @@ def tile_list_ownboard_bank_further_tabled_kernel(
                 diff[:, PACK - 1, js], board[PACK - 1][:].indirect(l4[:, h * 8 : (h + 1) * 8]),
                 a_sb[PACK - 1][:, js], ALU.subtract,
             )
+        nc.vector.tensor_copy(tz_g[:, 0, :], tz_t[:, 0, :].indirect(l6[:]))
         for h in range(2):
             js = slice(h * HALF, (h + 1) * HALF)
             hid = new("hid%d" % h, [P, HALF, PACK], BF16)
-            nc.scalar.activation(hid[:], diff[:, :, js].rearrange("p t j -> p j t"), ACT.Abs)
+            nc.scalar.activation(
+                hid[:].rearrange("p (c i) t -> p c t i", i=4),
+                diff[:, :, js].rearrange("p t (c i) -> p c t i", i=4), ACT.Abs,
+            )
             hq = new("hq%d" % h, [P, HALF], U32)
             hs = new("hs%d" % h, [P, HALF], U8)
             nc.vector.quantize_mx(hq[:].bitcast(E4M3), hs[:], hid[:].rearrange("p j t -> p (j t)"))

@@ -154,14 +154,14 @@ def tile_list_ownboard_bank_further_tabled_kernel(
         nc.vector.tensor_copy(stage2[:, 0:J].bitcast(I32), g5_s[:].bitcast(I32))
         deal(plane2, stage2, (nc.sync,))
 
-        p_ps = [psum.tile([P, 2, HALF], F32, name="p_ps%d" % h) for h in range(2)]
+        p_ps = [[psum.tile([P, HALF], F32, name="p_ps%d%d" % (h, c)) for c in range(2)] for h in range(2)]
         for h in range(2):
             js = slice(h * HALF, (h + 1) * HALF)
             for c in range(2):
                 nc.tensor.matmul_mx(
-                    p_ps[h][:, c, :], lhsT=ws_w[:, c * P : (c + 1) * P].bitcast(E5M2),
+                    p_ps[h][c][:], lhsT=ws_w[:, c * P : (c + 1) * P].bitcast(E5M2),
                     lhsT_scale=plane2[:, J + N + c * P : J + N + (c + 1) * P],
-                    rhs=g5_w[:, js].bitcast(E4M3), rhs_scale=plane2[:, js], start=(c == 0), stop=False,
+                    rhs=g5_w[:, js].bitcast(E4M3), rhs_scale=plane2[:, js], start=True, stop=False,
                 )
 
         a_sb = [new("a_sb%d" % t, [P, J], F32) for t in range(PACK)]
@@ -176,16 +176,16 @@ def tile_list_ownboard_bank_further_tabled_kernel(
         nc.scalar.copy(a_sb[0][:], a_ps[0][:])
         put_scalar(0)
         nc.vector.tensor_copy(a_sb[1][:], a_ps[1][:])
-        nc.vector.tensor_copy(board[1][:].indirect(l3[:]), a_sb[1][:])
-        nc.scalar.copy(a_sb[2][:], a_ps[2][:])
-        put_scalar(2)
+        put_scalar(1)
+        nc.vector.tensor_copy(a_sb[2][:], a_ps[2][:])
+        nc.vector.tensor_copy(board[2][:].indirect(l3[:]), a_sb[2][:])
         nc.vector.tensor_copy(a_sb[3][:], a_ps[3][:])
         put_scalar(3)
         for t in range(PACK - 1):
             look(t)
 
-        tz_g = new("tz_g", [P, 2, J], F32, tag="board2")
-        nc.scalar.activation(tz_g[:, 1, :], tz_t[:, 1, :].indirect(l6[:]), ACT.Copy)
+        hid = new("hid", [P, J, PACK], BF16)
+        nc.scalar.activation(hid[:, :, 0:2], diff[:, 0:2, :].rearrange("p t j -> p j t"), ACT.Abs)
         out_v = out.rearrange("(c p) j -> p c j", p=P)
         for h in range(2):
             js = slice(h * HALF, (h + 1) * HALF)
@@ -193,23 +193,28 @@ def tile_list_ownboard_bank_further_tabled_kernel(
                 diff[:, PACK - 1, js], board[PACK - 1][:].indirect(l4[:, h * 8 : (h + 1) * 8]),
                 a_sb[PACK - 1][:, js], ALU.subtract,
             )
-        nc.vector.tensor_copy(tz_g[:, 0, :], tz_t[:, 0, :].indirect(l6[:]))
+            nc.scalar.activation(hid[:, js, 2:4], diff[:, 2:4, js].rearrange("p t j -> p j t"), ACT.Abs)
+        tz_late = new("tz_late", [P, 3, HALF], F32, tag="board3")
+        nc.scalar.activation(tz_late[:, 2, :], tz_t[:, 1, :].indirect(l6[:, 0:8]), ACT.Copy)
+        for c in range(2):
+            nc.scalar.activation(tz_late[:, c, :], tz_t[:, c, :].indirect(l6[:, 8:16]), ACT.Copy)
+        tz_00 = new("tz_00", [P, HALF], F32, tag="a_sb3")
+        nc.vector.tensor_copy(tz_00[:], tz_t[:, 0, :].indirect(l6[:, 0:8]))
         for h in range(2):
             js = slice(h * HALF, (h + 1) * HALF)
-            hid = new("hid%d" % h, [P, HALF, PACK], BF16)
-            nc.scalar.activation(
-                hid[:].rearrange("p (c i) t -> p c t i", i=4),
-                diff[:, :, js].rearrange("p t (c i) -> p c t i", i=4), ACT.Abs,
-            )
             hq = new("hq%d" % h, [P, HALF], U32)
             hs = new("hs%d" % h, [P, HALF], U8)
-            nc.vector.quantize_mx(hq[:].bitcast(E4M3), hs[:], hid[:].rearrange("p j t -> p (j t)"))
+            nc.vector.quantize_mx(hq[:].bitcast(E4M3), hs[:], hid[:, js, :].rearrange("p j t -> p (j t)"))
             for c in range(2):
                 nc.tensor.matmul_mx(
-                    p_ps[h][:, c, :], lhsT=wb_w[:, c * P : (c + 1) * P].bitcast(E5M2),
+                    p_ps[h][c][:], lhsT=wb_w[:, c * P : (c + 1) * P].bitcast(E5M2),
                     lhsT_scale=plane2[:, J + c * P : J + (c + 1) * P],
-                    rhs=hq[:].bitcast(E4M3), rhs_scale=hs[:], start=False, stop=(c == 1),
+                    rhs=hq[:].bitcast(E4M3), rhs_scale=hs[:], start=False, stop=True,
                 )
-            res = new("res%d" % h, [P, 2, HALF], F32)
-            nc.vector.tensor_tensor(res[:], p_ps[h][:], tz_g[:, :, js], ALU.add)
+        tz_g = [[tz_00[:], tz_late[:, 2, :]], [tz_late[:, 0, :], tz_late[:, 1, :]]]
+        for h in range(2):
+            js = slice(h * HALF, (h + 1) * HALF)
+            res = new("res%d" % h, [P, 2, HALF], F32, tag="hid" if h == 0 else None)
+            for c in range(2):
+                nc.vector.tensor_tensor(res[:, c, :], p_ps[h][c][:], tz_g[h][c], ALU.add)
             nc.sync.dma_start(out_v[:, :, js], res[:])

from contextlib import ExitStack

import concourse.mybir as mybir

K, F, T, Z, J, R, C, N, E = 512, 512, 1024, 1024, 256, 512, 512, 256, 1024
FLOPS = 2 * J * (K * R + F * R + R * N + K * N)

F32 = mybir.dt.float32
BF16 = mybir.dt.bfloat16
I32 = mybir.dt.int32
U32 = mybir.dt.uint32
U16 = mybir.dt.uint16
U8 = mybir.dt.uint8
E4M3 = mybir.dt.float8_e4m3fn_x4
E5M2 = mybir.dt.float8_e5m2_x4
E2M1 = mybir.dt.float4_e2m1fn_x4
ACT = mybir.ActivationFunctionType
ALU = mybir.AluOpType

P = 128
PACK = 4
ROWS = 16
TOP = 96
HALF = J // 2


def tile_list_ownboard_bank_further_tabled_kernel(
    tc, xt_words, xt_scales, w_words, w_scales, xo_words, xo_scales, w0_words, w0_scales,
    wb_words, wb_scales, ws_words, ws_scales, tz, offs, offs2, offs3, offs4, offs5, offs6, out,
):
    nc = tc.nc

    def words32(ap):
        return ap[0].rearrange("p n t -> p (n t)").bitcast(I32)

    def twice(ap):
        rows = ap[0].bitcast(I32)
        return rows.unsqueeze(1).to_broadcast([ROWS, 2, rows.shape[1]])

    with ExitStack() as ctx:
        lists = ctx.enter_context(tc.tile_pool(name="lists", bufs=1))
        sb = ctx.enter_context(tc.tile_pool(name="sb", bufs=1))
        psum = ctx.enter_context(tc.psum_pool(name="psum", bufs=1))

        def new(name, shape, dtype, tag=None):
            return sb.tile(shape, dtype, name=name, tag=tag or name, align_bytes=64)

        def load_list(name, ap):
            tile = lists.tile([P, J // 16], U16, name=name)
            nc.sync.dma_start(tile[:], ap)
            return tile

        xt_s = new("xt_s", [P, T], U8)
        xo_s = new("xo_s", [P, Z], U8)
        w_raw = new("w_raw", [P, 2, R], U8)
        xt_w = new("xt_w", [P, T], U32)
        xo_w = new("xo_w", [P, Z], U16)
        w_w = new("w_w", [P, R], U16)
        w0_w = new("w0_w", [P, R], U32)
        wb_w = new("wb_w", [P, N], U32)
        ws_w = new("ws_w", [P, N], U32)
        stage1 = new("stage1", [P, 2 * J + R], U8)
        plane1 = new("plane1", [P, 2 * J + R], U8)
        plane1b = new("plane1b", [P, R], U8)
        stage2 = new("stage2", [P, J + 2 * N], U8)
        plane2 = new("plane2", [P, J + 2 * N], U8)
        board = [new("board%d" % t, [P, C], F32) for t in range(PACK)]

        nc.gpsimd.memset(xt_s[0:TOP, :].bitcast(I32), 0)
        nc.gpsimd.memset(xo_s[0:TOP, :].bitcast(I32), 0)
        nc.gpsimd.memset(w_raw[0:TOP].rearrange("p w r -> p (w r)").bitcast(I32), 0)
        nc.vector.memset(plane1[:].bitcast(I32), 0)
        nc.vector.memset(plane1b[:].bitcast(I32), 0)
        for t in range(2):
            nc.vector.memset(board[t][:], 0.0)

        l1 = load_list("l1", offs)
        nc.scalar.dma_start(xt_s[TOP:P, :].bitcast(I32), twice(xt_scales))
        nc.sync.dma_start(w_raw[TOP:P, 0, :].bitcast(I32), twice(w_scales))
        nc.scalar.dma_start(xo_s[TOP:P, :].bitcast(I32), twice(xo_scales))
        l2 = load_list("l2", offs2)
        nc.scalar.dma_start(w_raw[TOP:P, 1, :].bitcast(I32), twice(w0_scales))
        nc.sync.dma_start(xt_w[:].bitcast(I32), words32(xt_words))
        nc.scalar.dma_start(w_w[:].bitcast(I32), w_words[0].bitcast(I32))
        nc.sync.dma_start(w0_w[:].bitcast(I32), words32(w0_words))
        nc.sync.dma_start(xo_w[:].bitcast(I32), xo_words[0].bitcast(I32))
        l5 = load_list("l5", offs5)
        l3 = load_list("l3", offs3)
        nc.gpsimd.dma_start(stage2[TOP:P:2, J : J + N].bitcast(I32), wb_scales[0].bitcast(I32))
        nc.gpsimd.dma_start(stage2[TOP:P:2, J + N :].bitcast(I32), ws_scales[0].bitcast(I32))
        for t in range(2, PACK):
            nc.gpsimd.memset(board[t][:], 0.0)
        nc.gpsimd.dma_start(ws_w[:].bitcast(I32), words32(ws_words))
        nc.gpsimd.dma_start(wb_w[:].bitcast(I32), words32(wb_words))
        nc.gpsimd.memset(plane2[:].bitcast(I32), 0)

        def gather(name, window, offsets, dtype):
            tile = new(name, [P, J], dtype)
            nc.vector.tensor_copy(tile[:], window[:].indirect(offsets[:]))
            return tile

        def deal(plane, stage, queues):
            for q in range(4):
                queues[q % len(queues)].dma_start(
                    plane[32 * q : 32 * q + 4, :].bitcast(I32),
                    stage[TOP + 8 * q : TOP + 8 * q + 8 : 2, :].bitcast(I32),
                )

        w_p = new("w_p", [P, R], U16)
        nc.scalar.copy(w_p[:].rearrange("p (t m) -> p m t", t=PACK), w_w[:].rearrange("p (m t) -> p m t", t=PACK))
        by_t = w_raw[:].rearrange("p w (m t) -> p w t m", t=PACK)
        g_s = new("g_s", [P, 2 * J], U8)
        nc.vector.tensor_copy(g_s[:, 0:J], xt_s[:].indirect(l1[:]))
        nc.vector.tensor_copy(g_s[:, J:], xo_s[:].indirect(l2[:]))
        nc.vector.tensor_copy(stage1[:, 2 * J :].rearrange("p (w t m) -> p w t m", w=2, t=2), by_t[:, :, 0:2, :])
        nc.vector.tensor_copy(stage1[:, 0 : 2 * J].bitcast(I32), g_s[:].bitcast(I32))
        deal(plane1, stage1, (nc.scalar, nc.sync))
        stage1b = new("stage1b", [P, R], U8, tag="g_s")
        nc.vector.tensor_copy(stage1b[:].rearrange("p (w t m) -> p w t m", w=2, t=2), by_t[:, :, 2:4, :])
        deal(plane1b, stage1b, (nc.sync,))
        tz_t = new("tz_t", [P, 2, E], F32)
        nc.sync.dma_start(tz_t[:, 1, :], tz[P : 2 * P, :])
        l6 = load_list("l6", offs6)
        l4 = load_list("l4", offs4)
        nc.sync.dma_start(tz_t[:, 0, :], tz[0:P, :])

        g_xt_w = gather("g_xt_w", xt_w, l1, U32)
        g_xo_w = gather("g_xo_w", xo_w, l2, U16)

        w0_p = new("w0_p", [P, R], U32)
        nc.scalar.copy(w0_p[:].rearrange("p (t m) -> p m t", t=PACK), w0_w[:].rearrange("p (m t) -> p m t", t=PACK))

        def w_plane(which, t):
            at = which * 2 * P + (t % 2) * P
            return plane1[:, 2 * J + at : 2 * J + at + P] if t < 2 else plane1b[:, at : at + P]

        a_ps = []
        for t in range(PACK):
            acc = psum.tile([P, J], F32, name="a_ps%d" % t)
            cols = slice(t * P, (t + 1) * P)
            nc.tensor.matmul_mx(
                acc[:], lhsT=w_p[:, cols].bitcast(E2M1), lhsT_scale=w_plane(0, t),
                rhs=g_xt_w[:].bitcast(E4M3), rhs_scale=plane1[:, 0:J], start=True, stop=False,
            )
            nc.tensor.matmul_mx(
                acc[:], lhsT=w0_p[:, cols].bitcast(E5M2),
                lhsT_scale=w_plane(1, t),
                rhs=g_xo_w[:].bitcast(E2M1), rhs_scale=plane1[:, J : 2 * J], start=False, stop=True,
            )
            a_ps.append(acc)

        g5_s = gather("g5_s", xt_s, l5, U8)
        g5_w = gather("g5_w", xt_w, l5, U32)
        nc.vector.tensor_copy(stage2[:, 0:J].bitcast(I32), g5_s[:].bitcast(I32))
        deal(plane2, stage2, (nc.sync,))

        p_ps = [[psum.tile([P, HALF], F32, name="p_ps%d%d" % (h, c)) for c in range(2)] for h in range(2)]
        for h in range(2):
            js = slice(h * HALF, (h + 1) * HALF)
            for c in range(2):
                nc.tensor.matmul_mx(
                    p_ps[h][c][:], lhsT=ws_w[:, c * P : (c + 1) * P].bitcast(E5M2),
                    lhsT_scale=plane2[:, J + N + c * P : J + N + (c + 1) * P],
                    rhs=g5_w[:, js].bitcast(E4M3), rhs_scale=plane2[:, js], start=True, stop=False,
                )

        a_sb = [new("a_sb%d" % t, [P, J], F32) for t in range(PACK)]
        diff = new("diff", [P, PACK, J], F32)

        def put_scalar(t):
            nc.scalar.activation(board[t][:].indirect(l3[:]), a_sb[t][:], ACT.Copy)

        def look(t):
            nc.vector.tensor_tensor(diff[:, t, :], board[t][:].indirect(l4[:]), a_sb[t][:], ALU.subtract)

        nc.scalar.copy(a_sb[0][:], a_ps[0][:])
        put_scalar(0)
        nc.vector.tensor_copy(a_sb[1][:], a_ps[1][:])
        put_scalar(1)
        nc.vector.tensor_copy(a_sb[2][:], a_ps[2][:])
        nc.vector.tensor_copy(board[2][:].indirect(l3[:]), a_sb[2][:])
        nc.vector.tensor_copy(a_sb[3][:], a_ps[3][:])
        put_scalar(3)
        for t in range(PACK - 1):
            look(t)

        hid = new("hid", [P, J, PACK], BF16)
        nc.scalar.activation(hid[:, :, 0:2], diff[:, 0:2, :].rearrange("p t j -> p j t"), ACT.Abs)
        out_v = out.rearrange("(c p) j -> p c j", p=P)
        for h in range(2):
            js = slice(h * HALF, (h + 1) * HALF)
            nc.vector.tensor_tensor(
                diff[:, PACK - 1, js], board[PACK - 1][:].indirect(l4[:, h * 8 : (h + 1) * 8]),
                a_sb[PACK - 1][:, js], ALU.subtract,
            )
            nc.scalar.activation(hid[:, js, 2:4], diff[:, 2:4, js].rearrange("p t j -> p j t"), ACT.Abs)
        tz_late = new("tz_late", [P, 3, HALF], F32, tag="board3")
        nc.scalar.activation(tz_late[:, 2, :], tz_t[:, 1, :].indirect(l6[:, 0:8]), ACT.Copy)
        for c in range(2):
            nc.scalar.activation(tz_late[:, c, :], tz_t[:, c, :].indirect(l6[:, 8:16]), ACT.Copy)
        tz_00 = new("tz_00", [P, HALF], F32, tag="a_sb3")
        nc.vector.tensor_copy(tz_00[:], tz_t[:, 0, :].indirect(l6[:, 0:8]))
        for h in range(2):
            js = slice(h * HALF, (h + 1) * HALF)
            hq = new("hq%d" % h, [P, HALF], U32)
            hs = new("hs%d" % h, [P, HALF], U8)
            nc.vector.quantize_mx(hq[:].bitcast(E4M3), hs[:], hid[:, js, :].rearrange("p j t -> p (j t)"))
            for c in range(2):
                nc.tensor.matmul_mx(
                    p_ps[h][c][:], lhsT=wb_w[:, c * P : (c + 1) * P].bitcast(E5M2),
                    lhsT_scale=plane2[:, J + c * P : J + (c + 1) * P],
                    rhs=hq[:].bitcast(E4M3), rhs_scale=hs[:], start=False, stop=True,
                )
        tz_g = [[tz_00[:], tz_late[:, 2, :]], [tz_late[:, 0, :], tz_late[:, 1, :]]]
        for h in range(2):
            js = slice(h * HALF, (h + 1) * HALF)
            res = new("res%d" % h, [P, 2, HALF], F32, tag="hid" if h == 0 else None)
            for c in range(2):
                nc.vector.tensor_tensor(res[:, c, :], p_ps[h][c][:], tz_g[h][c], ALU.add)
            nc.sync.dma_start(out_v[:, :, js], res[:])
